import numpy as np
import ml_dtypes


def mxq(x, axis, fmt="e4m3"):
    dtype, down = {"e4m3": (ml_dtypes.float8_e4m3fn, 7), "e5m2": (ml_dtypes.float8_e5m2, 14)}[fmt]
    v = np.moveaxis(np.asarray(x, np.float32).astype(ml_dtypes.bfloat16).astype(np.float64), axis, -1)
    blocks = v.reshape(v.shape[:-1] + (-1, 32))
    amax = np.abs(blocks).max(-1, keepdims=True)
    byte = np.maximum(np.where(amax > 0, np.frexp(amax)[1] - 1 + 127, 0) - down, 1)
    scale = np.exp2(byte - 127.0)
    codes = (blocks / scale).astype(np.float32).astype(dtype).astype(np.float64)
    return np.moveaxis((codes * scale).reshape(v.shape), -1, axis)


WIDE = False


def mx_kscale(k):
    if not WIDE:
        return np.ones(k)
    levels = np.array([10, -10, 5, -5, 0])
    if k % 512:
        return np.exp2(np.random.permutation(np.resize(levels, k // 32))).repeat(32)
    a = np.empty((k // 512, 16))
    for p in range(k // 512):
        a[p, :8] = np.random.permutation(np.resize(levels, 8))
        for g in range(8):
            far = levels[np.abs(levels - a[p, g]) >= 10]
            a[p, g + 8] = far[np.random.randint(len(far))]
    return np.exp2(a.ravel()).repeat(32)


def f64(x):
    return np.asarray(x).astype(np.float64)


def striped(idx):
    return np.tile(idx.reshape(-1, 16).T, (8, 1)).astype(np.uint16)


def unstriped(offs):
    return offs[:16].T.reshape(-1).astype(np.int64)


E2M1 = np.array([0.0, 0.5, 1.0, 1.5, 2.0, 3.0, 4.0, 6.0, -0.0, -0.5, -1.0, -1.5, -2.0, -3.0, -4.0, -6.0])


def pack_weight(w, fmt):
    k, n = w.shape
    w = f64(np.asarray(w, np.float32).astype(ml_dtypes.bfloat16)).reshape(k // 32, 32, n)
    amax = np.abs(w).max(1)
    if fmt == "e4m3":
        byte = np.frexp(amax)[1] - 1 + 127 - 7
    else:
        mant, ex = np.frexp(amax / 6.0)
        byte = np.where(mant > 0.5, ex, ex - 1) + 127
    byte = np.clip(np.where(amax > 0, byte, 1), 1, 254)
    scaled = (w * np.exp2(127.0 - byte)[:, None, :]).reshape(k, n).astype(np.float32)
    by_word = np.ascontiguousarray(scaled.reshape(k // 512, 128, 4, n).transpose(0, 1, 3, 2))
    if fmt == "e4m3":
        words = by_word.astype(ml_dtypes.float8_e4m3fn).view(np.uint8)
    else:
        c = by_word.astype(ml_dtypes.float4_e2m1fn).view(np.uint8) & 0xF
        words = (c[..., 0::2] | (c[..., 1::2] << 4)).reshape(k // 512, 128, 2 * n)
    return np.ascontiguousarray(words), np.ascontiguousarray(byte.astype(np.uint8).reshape(k // 512, 16, n))


def unpack_weight(words, scales, fmt):
    g, _, n = scales.shape
    words = np.ascontiguousarray(words).reshape(g, 128, n, -1)
    if fmt == "e4m3":
        vals = words.view(ml_dtypes.float8_e4m3fn).astype(np.float64)
    else:
        nib = np.empty((g, 128, n, 4), np.uint8)
        nib[..., 0::2] = words & 0xF
        nib[..., 1::2] = words >> 4
        vals = E2M1[nib]
    vals = vals * np.repeat(np.exp2(scales.astype(np.float64) - 127.0), 8, axis=1)[..., None]
    return vals.transpose(0, 1, 3, 2).reshape(g * 512, n)


def gelu(v):
    return 0.5 * v * (1.0 + np.tanh(np.sqrt(2.0 / np.pi) * (v + 0.044715 * v**3)))


K, T, S, H, T3, S2 = 1536, 2048, 512, 1024, 2048, 512

def setup_inputs():
    n = np.random.standard_normal
    s = mx_kscale(K)[:, None]
    u = mx_kscale(H)[:, None]
    tab_words, tab_scales = pack_weight(n((K, T)) * s, "e4m3")
    tab2_words, tab2_scales = pack_weight(n((H, T3)) / np.sqrt(H) / u, "e4m3")
    tab3_words, tab3_scales = pack_weight(n((H, T3)) / np.sqrt(H) / u, "e4m3")
    w2_words, w2_scales = pack_weight(n((K, H)) / np.sqrt(K) / s * u.T, "e2m1")
    return {
        "tab_words": tab_words, "tab_scales": tab_scales,
        "offs": striped(np.random.permutation(T)[:S]),
        "tab2_words": tab2_words, "tab2_scales": tab2_scales,
        "offs2": striped(np.random.permutation(T3)[:S2]),
        "tab3_words": tab3_words, "tab3_scales": tab3_scales,
        "offs3": striped(np.random.permutation(T3)[:S2]),
        "w1": (n((K, H)) / np.sqrt(K) / s * u.T).astype(np.float32),
        "b1": (0.5 * n(H) * u[:, 0]).astype(np.float32),
        "w2_words": w2_words, "w2_scales": w2_scales,
        "w3": (n((K, S2)) / np.sqrt(K) / s).astype(np.float32),
        "gain": np.exp(0.3 * n(S2)).astype(np.float32),
    }

def reference(tab_words, tab_scales, offs, tab2_words, tab2_scales, offs2, tab3_words, tab3_scales, offs3,
              w1, b1, w2_words, w2_scales, w3, gain):
    v = unpack_weight(tab_words, tab_scales, "e4m3")[:, unstriped(offs)]
    v2 = unpack_weight(tab2_words, tab2_scales, "e4m3")[:, unstriped(offs2)]
    v3 = unpack_weight(tab3_words, tab3_scales, "e4m3")[:, unstriped(offs3)]
    w2 = unpack_weight(w2_words, w2_scales, "e2m1")
    x1 = (mxq(f64(w1), 0, "e4m3").T @ v) + f64(b1)[:, None]
    x2 = w2.T @ v
    h = mxq(np.maximum(x1, x2), 0, "e4m3")
    e2 = v2.T @ h + mxq(f64(w3), 0, "e4m3").T @ v
    e3 = v3.T @ h
    return np.maximum(np.tanh(e2), e3) * f64(gain)[:, None]

@@ -1,0 +1,292 @@
+from contextlib import ExitStack
+
+import concourse.mybir as mybir
+
+K, T, S, H, S2 = 1536, 2048, 512, 1024, 512
+FLOPS = 2 * (2 * K * H * S + 2 * H * S2 * S + K * S2 * S)
+
+F32 = mybir.dt.float32
+BF16 = mybir.dt.bfloat16
+I32 = mybir.dt.int32
+U32 = mybir.dt.uint32
+U16 = mybir.dt.uint16
+U8 = mybir.dt.uint8
+FP8X4 = mybir.dt.float8_e4m3fn_x4
+FP4X4 = mybir.dt.float4_e2m1fn_x4
+ALU = mybir.AluOpType
+ACT = mybir.ActivationFunctionType
+
+P = 128
+PACK = 4
+K_PASS = P * PACK
+K_PASSES = K // K_PASS
+H_PASSES = H // K_PASS
+M_TILES = S2 // P
+LIVE_ROWS = 100
+RAW_BUFS = 6
+VECTOR_QUADS = 40
+
+
+def tile_list_bid_pair_board_kernel(
+    tc, tab_words, tab_scales, offs, tab2_words, tab2_scales, offs2, tab3_words, tab3_scales, offs3,
+    w1, b1, w2_words, w2_scales, w3, gain, out,
+):
+    nc = tc.nc
+    with ExitStack() as ctx:
+        keep = ctx.enter_context(tc.tile_pool(name="keep", bufs=1))
+        raw_pool = ctx.enter_context(tc.tile_pool(name="raw", bufs=RAW_BUFS))
+        stage = ctx.enter_context(tc.tile_pool(name="stage", bufs=3))
+        psum = ctx.enter_context(tc.psum_pool(name="psum", bufs=1))
+
+        def held(shape, dtype, name):
+            return keep.tile(shape, dtype, name=name, align_bytes=64)
+
+        def bank(group, index):
+            return psum.tile([P, S], F32, name="bank_%s%d" % (group, index))
+
+        def load_list(source, name):
+            listed = keep.tile([P, S // 16], U16, name=name)
+            nc.sync.dma_start(listed[:], source)
+            return listed
+
+        def load_words(words, a, name):
+            window = held([P, T], I32, name)
+            nc.sync.dma_start(out=window[:], in_=words[a].rearrange("p t i -> p (t i)").bitcast(I32))
+            return window
+
+        def load_weight(w, a, b):
+            raw = raw_pool.tile([P, PACK, K_PASS], F32, name="raw")
+            rows = w[a * K_PASS : (a + 1) * K_PASS, b * K_PASS : (b + 1) * K_PASS]
+            nc.sync.dma_start(out=raw[:], in_=rows.rearrange("(p j) c -> p j c", j=PACK))
+            return raw
+
+        def zeroed(width, name):
+            planes = held([P, width], U8, name)
+            nc.vector.memset(planes[:].bitcast(I32), 0)
+            return planes
+
+        def load_planes(planes, scales, first_row):
+            rows = 4 * scales.shape[0]
+            for q in range(4):
+                start = 32 * q + first_row
+                nc.gpsimd.dma_start(
+                    out=planes[start : start + rows, :].bitcast(I32),
+                    in_=scales[:, 4 * q : 4 * q + 4, :].bitcast(I32),
+                )
+
+        def move_plane_down(target, planes, a):
+            nc.gpsimd.dma_start(
+                out=target[0:LIVE_ROWS, :].bitcast(I32),
+                in_=planes[4 * a : 4 * a + LIVE_ROWS, :].bitcast(I32),
+            )
+
+        def gather_words(window, listed, name, pieces=1):
+            picked = held([P, S], U32, name)
+            step = S // pieces
+            for u in range(pieces):
+                part = listed[:, u * step // 16 : (u + 1) * step // 16]
+                nc.vector.tensor_copy(picked[:, u * step : (u + 1) * step], window[:].bitcast(U32).indirect(part))
+            return picked
+
+        def gather_planes(planes, listed, name):
+            picked = held([P, S], U8, name)
+            nc.vector.tensor_copy(picked[:], planes[:].indirect(listed[:]))
+            return picked
+
+        def round_weight(raw, dealt, vector_quads):
+            grouped = stage.tile([P, K_PASS * PACK], BF16, name="grouped", align_bytes=64)
+            source = raw[:].rearrange("p j (m t) -> p m j t", t=PACK)
+            if dealt:
+                target = grouped[:].rearrange("p (t m j) -> p m j t", t=PACK, j=PACK)
+            else:
+                target = grouped[:].rearrange("p (m t j) -> p m j t", t=PACK, j=PACK)
+            cut = P - vector_quads
+            nc.scalar.copy(out=target[:, 0:cut], in_=source[:, 0:cut])
+            if vector_quads:
+                nc.vector.tensor_copy(out=target[:, cut:P], in_=source[:, cut:P])
+            return grouped
+
+        def quantise(grouped, name):
+            codes = held([P, K_PASS], U32, name + "_codes")
+            plane = held([P, K_PASS], U8, name + "_plane")
+            nc.vector.quantize_mx(out=codes[:].bitcast(FP8X4), scales=plane[:], in_=grouped[:])
+            return codes, plane
+
+        def mx(acc, lhs, lhs_plane, rhs, rhs_plane, start, stop):
+            nc.tensor.matmul_mx(
+                out=acc[:], lhsT=lhs, lhsT_scale=lhs_plane, rhs=rhs, rhs_scale=rhs_plane, start=start, stop=stop
+            )
+
+        def cols(index):
+            return slice(index * P, (index + 1) * P)
+
+        tab_planes = zeroed(T, "tab_planes")
+        w2_planes_raw = zeroed(H, "w2_planes_raw")
+        tab2_planes = zeroed(T, "tab2_planes")
+        tab3_planes = zeroed(T, "tab3_planes")
+        v_low = [None] + [zeroed(S, "v_low%d" % a) for a in range(1, K_PASSES)]
+        w2_low = [None] + [zeroed(H, "w2_low%d" % a) for a in range(1, K_PASSES)]
+
+        w1_raw = {}
+        tab_win = []
+        w1_raw[0, 0] = load_weight(w1, 0, 0)
+        list1 = load_list(offs, "list1")
+        tab_win.append(load_words(tab_words, 0, "tab_win0"))
+        w1_raw[1, 0] = load_weight(w1, 1, 0)
+        w2_raw = held([P, K_PASSES, H // 2], I32, "w2_raw")
+        nc.sync.dma_start(out=w2_raw[:], in_=w2_words.bitcast(I32).rearrange("a p n -> p a n"))
+        tab_win.append(load_words(tab_words, 1, "tab_win1"))
+        w1_raw[2, 0] = load_weight(w1, 2, 0)
+        list2 = load_list(offs2, "list2")
+        list3 = load_list(offs3, "list3")
+        tab_win.append(load_words(tab_words, 2, "tab_win2"))
+        bias = keep.tile([P, H_PASSES, PACK], F32, name="bias")
+        nc.sync.dma_start(out=bias[:], in_=b1.rearrange("(b p t) -> p b t", p=P, t=PACK))
+        for a in range(K_PASSES):
+            w1_raw[a, 1] = load_weight(w1, a, 1)
+        gains = keep.tile([P, M_TILES], F32, name="gains")
+        with nc.allow_non_contiguous_dma(reason="one gain for each output row"):
+            nc.sync.dma_start(out=gains[:], in_=gain.rearrange("(u p) -> p u", p=P))
+
+        load_planes(tab_planes, tab_scales, 0)
+        load_planes(w2_planes_raw, w2_scales, 0)
+        load_planes(tab2_planes, tab2_scales, 0)
+        load_planes(tab3_planes, tab3_scales, 8)
+
+        v_planes = gather_planes(tab_planes, list1, "v_planes")
+        v_low[0] = v_planes
+        w2_planes = held([P, H], U8, "w2_planes")
+        nc.vector.tensor_copy(
+            out=w2_planes[:].rearrange("p (t g i) -> p g t i", t=PACK, i=16),
+            in_=w2_planes_raw[:].rearrange("p (g i t) -> p g t i", t=PACK, i=16),
+        )
+        w2_low[0] = w2_planes
+        for a in range(1, K_PASSES):
+            move_plane_down(v_low[a], v_planes, a)
+            move_plane_down(w2_low[a], w2_planes, a)
+
+        v_codes = []
+        w1_q = {}
+        x1 = [bank("a", t) for t in range(PACK)]
+        w2_codes = held([P, PACK, K_PASSES * H // PACK * 2], U8, "w2_codes")
+
+        def x1_pass(a, b):
+            codes, plane = w1_q[a, b]
+            for t in range(PACK):
+                mx(x1[t], codes[:, cols(t)].bitcast(FP8X4), plane[:, cols(t)],
+                   v_codes[a][:].bitcast(FP8X4), v_planes[4 * a : P, :], a == 0, a == K_PASSES - 1)
+
+        def x2_pass(x2, a, b):
+            for t in range(PACK):
+                first = (a * H_PASSES + b) * 2 * P
+                mx(x2[t], w2_codes[:, t, first : first + 2 * P].bitcast(FP4X4), w2_low[a][:, cols(t * H_PASSES + b)],
+                   v_codes[a][:].bitcast(FP8X4), v_low[a][:], a == 0, a == K_PASSES - 1)
+
+        x2_first = [bank("b", t) for t in range(PACK)]
+        for a in range(K_PASSES):
+            grouped = round_weight(w1_raw[a, 0], True, 0)
+            v_codes.append(gather_words(tab_win[a], list1, "v_codes%d" % a))
+            w1_q[a, 0] = quantise(grouped, "w1_%d0" % a)
+            if a == 1:
+                nc.vector.tensor_copy(
+                    out=w2_codes[:].bitcast(U16).rearrange("p t (g i) -> p g t i", i=8),
+                    in_=w2_raw[:].rearrange("p a n -> p (a n)").bitcast(U16).rearrange("p (g i t) -> p g t i", t=PACK, i=8),
+                )
+            x1_pass(a, 0)
+        for a in range(K_PASSES):
+            x2_pass(x2_first, a, 0)
+
+        v2_planes = gather_planes(tab2_planes, list2, "v2_planes")
+        v3_planes = gather_planes(tab3_planes, list3, "v3_planes")
+
+        def empty_x2(x2, b):
+            kept = []
+            for t in range(PACK):
+                x2_sb = held([P, S], F32, "x2_sb%d%d" % (b, t))
+                nc.scalar.copy(out=x2_sb[:], in_=x2[t][:])
+                kept.append(x2_sb)
+            return kept
+
+        def larger_reading(x2_sb, b):
+            h_rows = held([P, PACK, S], BF16, "h_rows%d" % b)
+            for t in range(PACK):
+                nc.vector.scalar_tensor_tensor(
+                    out=h_rows[:, t, :], in0=x1[t][:], scalar=bias[:, b, t : t + 1], in1=x2_sb[t][:],
+                    op0=ALU.add, op1=ALU.max,
+                )
+            return h_rows
+
+        def interleave_h(h_rows):
+            grouped = stage.tile([P, K_PASS * PACK], BF16, name="grouped", align_bytes=64)
+            nc.vector.tensor_copy(
+                out=grouped[:].rearrange("p (c i t) -> p c t i", t=PACK, i=4),
+                in_=h_rows[:].rearrange("p t (c i) -> p c t i", i=4),
+            )
+            return grouped
+
+        x2_sb0 = empty_x2(x2_first, 0)
+        x2_second = [bank("b", t) for t in range(PACK)]
+        for a in range(K_PASSES):
+            x2_pass(x2_second, a, 1)
+        h_rows0 = larger_reading(x2_sb0, 0)
+
+        w3_raw = [load_weight(w3, 0, 0)]
+        tab2_win = [load_words(tab2_words, 0, "tab2_win0")]
+        w3_raw.append(load_weight(w3, 1, 0))
+        tab2_win.append(load_words(tab2_words, 1, "tab2_win1"))
+        w3_raw.append(load_weight(w3, 2, 0))
+        tab3_win = [load_words(tab3_words, a, "tab3_win%d" % a) for a in range(H_PASSES)]
+
+        x1 = [bank("a", t) for t in range(PACK)]
+        grouped = round_weight(w1_raw[0, 1], True, VECTOR_QUADS)
+        h_grouped0 = interleave_h(h_rows0)
+        w1_q[0, 1] = quantise(grouped, "w1_01")
+        x1_pass(0, 1)
+        x2_sb1 = empty_x2(x2_second, 1)
+        h_q = [quantise(h_grouped0, "h0")]
+        for a in range(1, K_PASSES):
+            grouped = round_weight(w1_raw[a, 1], True, VECTOR_QUADS)
+            w1_q[a, 1] = quantise(grouped, "w1_%d1" % a)
+            x1_pass(a, 1)
+
+        e2 = [bank("b", u) for u in range(M_TILES)]
+
+        def w3_pass(a, vector_quads, start, stop):
+            codes, plane = quantise(round_weight(w3_raw[a], False, vector_quads), "w3_%d" % a)
+            for u in range(M_TILES):
+                mx(e2[u], codes[:, cols(u)].bitcast(FP8X4), plane[:, cols(u)],
+                   v_codes[a][:].bitcast(FP8X4), v_planes[4 * a : P, :], start, stop)
+
+        def table_pass(acc, picked, planes, first_row, b, start, stop):
+            codes, plane = h_q[b]
+            for u in range(M_TILES):
+                mx(acc[u], picked[:, cols(u)].bitcast(FP8X4), planes[first_row + 4 * b : P, cols(u)],
+                   codes[:].bitcast(FP8X4), plane[:], start, stop)
+
+        h_rows1 = larger_reading(x2_sb1, 1)
+        w3_pass(0, VECTOR_QUADS, True, False)
+        h_grouped1 = interleave_h(h_rows1)
+        table_pass(e2, gather_words(tab2_win[0], list2, "v2_codes0"), v2_planes, 0, 0, False, False)
+        h_q.append(quantise(h_grouped1, "h1"))
+        w3_pass(1, VECTOR_QUADS, False, False)
+        table_pass(e2, gather_words(tab2_win[1], list2, "v2_codes1"), v2_planes, 0, 1, False, False)
+        w3_pass(2, VECTOR_QUADS, False, True)
+
+        e3 = [bank("a", u) for u in range(M_TILES)]
+        table_pass(e3, gather_words(tab3_win[0], list3, "v3_codes0"), v3_planes, 8, 0, True, False)
+        bounded = []
+        for u in range(M_TILES):
+            th = held([P, S], F32, "x2_sb0%d" % u)
+            nc.scalar.activation(out=th[:], in_=e2[u][:], func=ACT.Tanh)
+            bounded.append(th)
+        table_pass(e3, gather_words(tab3_win[1], list3, "v3_codes1", pieces=2), v3_planes, 8, 1, False, True)
+
+        for u in range(M_TILES):
+            larger = held([P, S], F32, "x2_sb1%d" % u)
+            nc.vector.tensor_tensor(out=larger[:], in0=e3[u][:], in1=bounded[u][:], op=ALU.max)
+            score = held([P, S], F32, "score%d" % u)
+            if u < M_TILES - 1:
+                nc.scalar.activation(out=score[:], in_=larger[:], func=ACT.Copy, scale=gains[:, u : u + 1])
+            else:
+                nc.vector.tensor_scalar(out=score[:], in0=larger[:], scalar1=gains[:, u : u + 1], scalar2=None, op0=ALU.mult)
+            nc.sync.dma_start(out=out[cols(u), :], in_=score[:])

@@ -22,9 +22,8 @@ K_PASS = P * PACK
 K_PASSES = K // K_PASS
 H_PASSES = H // K_PASS
 M_TILES = S2 // P
-LIVE_ROWS = 100
-RAW_BUFS = 6
-VECTOR_QUADS = 40
+RAW_BUFS = 8
+VECTOR_QUADS = 0
 
 
 def tile_list_bid_pair_board_kernel(
@@ -60,12 +59,19 @@ def tile_list_bid_pair_board_kernel(
             nc.sync.dma_start(out=raw[:], in_=rows.rearrange("(p j) c -> p j c", j=PACK))
             return raw
 
-        def zeroed(width, name):
-            planes = held([P, width], U8, name)
-            nc.vector.memset(planes[:].bitcast(I32), 0)
+        def zeroed(engine, shape, name):
+            planes = held(shape, U8, name)
+            engine.memset(planes[:].bitcast(I32), 0)
             return planes
 
-        def load_planes(planes, scales, first_row):
+        def load_planes_apart(planes, scales):
+            for q in range(4):
+                nc.sync.dma_start(
+                    out=planes[32 * q : 32 * q + 4, :, :].bitcast(I32),
+                    in_=scales[:, 4 * q : 4 * q + 4, :].bitcast(I32).rearrange("a r n -> r a n"),
+                )
+
+        def load_planes_packed(planes, scales, first_row):
             rows = 4 * scales.shape[0]
             for q in range(4):
                 start = 32 * q + first_row
@@ -73,12 +79,6 @@ def tile_list_bid_pair_board_kernel(
                     out=planes[start : start + rows, :].bitcast(I32),
                     in_=scales[:, 4 * q : 4 * q + 4, :].bitcast(I32),
                 )
-
-        def move_plane_down(target, planes, a):
-            nc.gpsimd.dma_start(
-                out=target[0:LIVE_ROWS, :].bitcast(I32),
-                in_=planes[4 * a : 4 * a + LIVE_ROWS, :].bitcast(I32),
-            )
 
         def gather_words(window, listed, name, pieces=1):
             picked = held([P, S], U32, name)
@@ -90,7 +90,7 @@ def tile_list_bid_pair_board_kernel(
 
         def gather_planes(planes, listed, name):
             picked = held([P, S], U8, name)
-            nc.vector.tensor_copy(picked[:], planes[:].indirect(listed[:]))
+            nc.vector.tensor_copy(picked[:], planes.indirect(listed[:]))
             return picked
 
         def round_weight(raw, dealt, vector_quads):
@@ -120,84 +120,119 @@ def tile_list_bid_pair_board_kernel(
         def cols(index):
             return slice(index * P, (index + 1) * P)
 
-        tab_planes = zeroed(T, "tab_planes")
-        w2_planes_raw = zeroed(H, "w2_planes_raw")
-        tab2_planes = zeroed(T, "tab2_planes")
-        tab3_planes = zeroed(T, "tab3_planes")
-        v_low = [None] + [zeroed(S, "v_low%d" % a) for a in range(1, K_PASSES)]
-        w2_low = [None] + [zeroed(H, "w2_low%d" % a) for a in range(1, K_PASSES)]
+        tab_planes = zeroed(nc.vector, [P, K_PASSES, T], "tab_planes")
+        w2_planes_raw = zeroed(nc.vector, [P, K_PASSES, H], "w2_planes_raw")
+        tab2_planes = zeroed(nc.gpsimd, [P, T], "tab2_planes")
+        load_planes_packed(tab2_planes, tab2_scales, 4)
+        tab3_planes = zeroed(nc.gpsimd, [P, T], "tab3_planes")
+        load_planes_packed(tab3_planes, tab3_scales, 8)
 
         w1_raw = {}
         tab_win = []
-        w1_raw[0, 0] = load_weight(w1, 0, 0)
-        list1 = load_list(offs, "list1")
         tab_win.append(load_words(tab_words, 0, "tab_win0"))
-        w1_raw[1, 0] = load_weight(w1, 1, 0)
+        list1 = load_list(offs, "list1")
+        load_planes_apart(tab_planes, tab_scales)
+        w1_raw[0, 0] = load_weight(w1, 0, 0)
+        load_planes_apart(w2_planes_raw, w2_scales)
         w2_raw = held([P, K_PASSES, H // 2], I32, "w2_raw")
         nc.sync.dma_start(out=w2_raw[:], in_=w2_words.bitcast(I32).rearrange("a p n -> p a n"))
         tab_win.append(load_words(tab_words, 1, "tab_win1"))
-        w1_raw[2, 0] = load_weight(w1, 2, 0)
-        list2 = load_list(offs2, "list2")
-        list3 = load_list(offs3, "list3")
+        w1_raw[1, 0] = load_weight(w1, 1, 0)
         tab_win.append(load_words(tab_words, 2, "tab_win2"))
+        w1_raw[2, 0] = load_weight(w1, 2, 0)
         bias = keep.tile([P, H_PASSES, PACK], F32, name="bias")
         nc.sync.dma_start(out=bias[:], in_=b1.rearrange("(b p t) -> p b t", p=P, t=PACK))
-        for a in range(K_PASSES):
-            w1_raw[a, 1] = load_weight(w1, a, 1)
+        w1_raw[0, 1] = load_weight(w1, 0, 1)
+        w1_raw[1, 1] = load_weight(w1, 1, 1)
+        list2 = load_list(offs2, "list2")
+        list3 = load_list(offs3, "list3")
+        w1_raw[2, 1] = load_weight(w1, 2, 1)
         gains = keep.tile([P, M_TILES], F32, name="gains")
         with nc.allow_non_contiguous_dma(reason="one gain for each output row"):
             nc.sync.dma_start(out=gains[:], in_=gain.rearrange("(u p) -> p u", p=P))
-
-        load_planes(tab_planes, tab_scales, 0)
-        load_planes(w2_planes_raw, w2_scales, 0)
-        load_planes(tab2_planes, tab2_scales, 0)
-        load_planes(tab3_planes, tab3_scales, 8)
-
-        v_planes = gather_planes(tab_planes, list1, "v_planes")
-        v_low[0] = v_planes
-        w2_planes = held([P, H], U8, "w2_planes")
-        nc.vector.tensor_copy(
-            out=w2_planes[:].rearrange("p (t g i) -> p g t i", t=PACK, i=16),
-            in_=w2_planes_raw[:].rearrange("p (g i t) -> p g t i", t=PACK, i=16),
-        )
-        w2_low[0] = w2_planes
-        for a in range(1, K_PASSES):
-            move_plane_down(v_low[a], v_planes, a)
-            move_plane_down(w2_low[a], w2_planes, a)
+        w3_raw = [load_weight(w3, 0, 0)]
+        tab2_win = [load_words(tab2_words, 0, "tab2_win0")]
+        w3_raw.append(load_weight(w3, 1, 0))
+        tab2_win.append(load_words(tab2_words, 1, "tab2_win1"))
+        w3_raw.append(load_weight(w3, 2, 0))
+        tab3_win = [load_words(tab3_words, a, "tab3_win%d" % a) for a in range(H_PASSES)]
 
         v_codes = []
+        v_planes = []
         w1_q = {}
-        x1 = [bank("a", t) for t in range(PACK)]
-        w2_codes = held([P, PACK, K_PASSES * H // PACK * 2], U8, "w2_codes")
 
-        def x1_pass(a, b):
+        def x1_pass(x1, a, b):
             codes, plane = w1_q[a, b]
             for t in range(PACK):
                 mx(x1[t], codes[:, cols(t)].bitcast(FP8X4), plane[:, cols(t)],
-                   v_codes[a][:].bitcast(FP8X4), v_planes[4 * a : P, :], a == 0, a == K_PASSES - 1)
+                   v_codes[a][:].bitcast(FP8X4), v_planes[a][:], a == 0, a == K_PASSES - 1)
 
         def x2_pass(x2, a, b):
+            block = a * H_PASSES + b
             for t in range(PACK):
-                first = (a * H_PASSES + b) * 2 * P
-                mx(x2[t], w2_codes[:, t, first : first + 2 * P].bitcast(FP4X4), w2_low[a][:, cols(t * H_PASSES + b)],
-                   v_codes[a][:].bitcast(FP8X4), v_low[a][:], a == 0, a == K_PASSES - 1)
+                mx(x2[t], w2_codes[:, t, block * 2 * P : (block + 1) * 2 * P].bitcast(FP4X4), w2_planes[:, t, cols(block)],
+                   v_codes[a][:].bitcast(FP8X4), v_planes[a][:], a == 0, a == K_PASSES - 1)
 
-        x2_first = [bank("b", t) for t in range(PACK)]
-        for a in range(K_PASSES):
-            grouped = round_weight(w1_raw[a, 0], True, 0)
-            v_codes.append(gather_words(tab_win[a], list1, "v_codes%d" % a))
-            w1_q[a, 0] = quantise(grouped, "w1_%d0" % a)
-            if a == 1:
-                nc.vector.tensor_copy(
-                    out=w2_codes[:].bitcast(U16).rearrange("p t (g i) -> p g t i", i=8),
-                    in_=w2_raw[:].rearrange("p a n -> p (a n)").bitcast(U16).rearrange("p (g i t) -> p g t i", t=PACK, i=8),
+        def x2_pass_by_quarters(x2, a, b):
+            block = a * H_PASSES + b
+            for q in range(PACK):
+                for t in range(PACK):
+                    nc.tensor.matmul_mx(
+                        out=x2[q][:, cols(t)],
+                        lhsT=w2_codes[:, t, block * 2 * P : (block + 1) * 2 * P].bitcast(FP4X4),
+                        lhsT_scale=w2_planes[:, t, cols(block)],
+                        rhs=v_codes[a][:, cols(q)].bitcast(FP8X4),
+                        rhs_scale=v_planes[a][:, cols(q)],
+                        start=(a == 0 and t == 0),
+                        stop=(a == K_PASSES - 1 and t == PACK - 1),
+                    )
+
+        def biased_x1(x1, b):
+            x1_sb = held([P, PACK, S], F32, "x1_sb")
+            for half in range(2):
+                span = slice(half * S // 2, (half + 1) * S // 2)
+                for t in range(PACK):
+                    nc.scalar.activation(
+                        out=x1_sb[:, t, span], in_=x1[t][:, span], func=ACT.Identity, bias=bias[:, b, t : t + 1]
+                    )
+            return x1_sb
+
+        def larger_interleaved(x2, x1_sb):
+            grouped = stage.tile([P, K_PASS * PACK], BF16, name="grouped", align_bytes=64)
+            for q in range(PACK):
+                nc.vector.tensor_tensor(
+                    out=grouped[:, q * K_PASS : (q + 1) * K_PASS].rearrange("p (c i t) -> p c t i", t=PACK, i=4),
+                    in0=x2[q][:].rearrange("p (t c i) -> p c t i", t=PACK, i=4),
+                    in1=x1_sb[:, :, cols(q)].rearrange("p t (c i) -> p c t i", i=4),
+                    op=ALU.max,
                 )
-            x1_pass(a, 0)
-        for a in range(K_PASSES):
-            x2_pass(x2_first, a, 0)
+            return grouped
 
-        v2_planes = gather_planes(tab2_planes, list2, "v2_planes")
-        v3_planes = gather_planes(tab3_planes, list3, "v3_planes")
+        x1_first = [bank("a", t) for t in range(PACK)]
+        v_codes.append(gather_words(tab_win[0], list1, "v_codes0"))
+        for a in range(K_PASSES):
+            v_planes.append(gather_planes(tab_planes[:, a, :], list1, "v_plane%d" % a))
+        w1_q[0, 0] = quantise(round_weight(w1_raw[0, 0], True, 0), "w1_00")
+        x1_pass(x1_first, 0, 0)
+        w2_planes = held([P, PACK, K_PASSES * H // PACK], U8, "w2_planes")
+        nc.vector.tensor_copy(
+            out=w2_planes[:].rearrange("p t (g i) -> p g t i", i=16),
+            in_=w2_planes_raw[:].rearrange("p a (g i t) -> p (a g) t i", t=PACK, i=16),
+        )
+        w2_codes = held([P, PACK, K_PASSES * H // PACK * 2], U8, "w2_codes")
+        nc.vector.tensor_copy(
+            out=w2_codes[:].bitcast(U16).rearrange("p t (g i) -> p g t i", i=8),
+            in_=w2_raw[:].rearrange("p a n -> p (a n)").bitcast(U16).rearrange("p (g i t) -> p g t i", t=PACK, i=8),
+        )
+        x2_second = [bank("b", t) for t in range(PACK)]
+        x2_pass(x2_second, 0, 1)
+        v_codes.append(gather_words(tab_win[1], list1, "v_codes1"))
+        x2_pass(x2_second, 1, 1)
+        grouped = round_weight(w1_raw[1, 0], True, 0)
+        v_codes.append(gather_words(tab_win[2], list1, "v_codes2"))
+        x2_pass(x2_second, 2, 1)
+        w1_q[1, 0] = quantise(grouped, "w1_10")
+        x1_pass(x1_first, 1, 0)
 
         def empty_x2(x2, b):
             kept = []
@@ -207,7 +242,7 @@ def tile_list_bid_pair_board_kernel(
                 kept.append(x2_sb)
             return kept
 
-        def larger_reading(x2_sb, b):
+        def larger_reading(x1, x2_sb, b):
             h_rows = held([P, PACK, S], BF16, "h_rows%d" % b)
             for t in range(PACK):
                 nc.vector.scalar_tensor_tensor(
@@ -224,30 +259,24 @@ def tile_list_bid_pair_board_kernel(
             )
             return grouped
 
-        x2_sb0 = empty_x2(x2_first, 0)
-        x2_second = [bank("b", t) for t in range(PACK)]
-        for a in range(K_PASSES):
-            x2_pass(x2_second, a, 1)
-        h_rows0 = larger_reading(x2_sb0, 0)
-
-        w3_raw = [load_weight(w3, 0, 0)]
-        tab2_win = [load_words(tab2_words, 0, "tab2_win0")]
-        w3_raw.append(load_weight(w3, 1, 0))
-        tab2_win.append(load_words(tab2_words, 1, "tab2_win1"))
-        w3_raw.append(load_weight(w3, 2, 0))
-        tab3_win = [load_words(tab3_words, a, "tab3_win%d" % a) for a in range(H_PASSES)]
-
-        x1 = [bank("a", t) for t in range(PACK)]
-        grouped = round_weight(w1_raw[0, 1], True, VECTOR_QUADS)
-        h_grouped0 = interleave_h(h_rows0)
-        w1_q[0, 1] = quantise(grouped, "w1_01")
-        x1_pass(0, 1)
         x2_sb1 = empty_x2(x2_second, 1)
+        w1_q[2, 0] = quantise(round_weight(w1_raw[2, 0], True, 2 * VECTOR_QUADS), "w1_20")
+        x1_pass(x1_first, 2, 0)
+        x2_first = [bank("b", t) for t in range(PACK)]
+        for a in range(K_PASSES):
+            x2_pass_by_quarters(x2_first, a, 0)
+        x1_sb = biased_x1(x1_first, 0)
+        x1_second = [bank("a", t) for t in range(PACK)]
+        w1_q[0, 1] = quantise(round_weight(w1_raw[0, 1], True, 2 * VECTOR_QUADS), "w1_01")
+        x1_pass(x1_second, 0, 1)
+        h_grouped0 = larger_interleaved(x2_first, x1_sb)
+        w1_q[1, 1] = quantise(round_weight(w1_raw[1, 1], True, VECTOR_QUADS), "w1_11")
+        x1_pass(x1_second, 1, 1)
         h_q = [quantise(h_grouped0, "h0")]
-        for a in range(1, K_PASSES):
-            grouped = round_weight(w1_raw[a, 1], True, VECTOR_QUADS)
-            w1_q[a, 1] = quantise(grouped, "w1_%d1" % a)
-            x1_pass(a, 1)
+        w1_q[2, 1] = quantise(round_weight(w1_raw[2, 1], True, VECTOR_QUADS), "w1_21")
+        x1_pass(x1_second, 2, 1)
+        v2_planes = gather_planes(tab2_planes[:], list2, "v2_planes")
+        v3_planes = gather_planes(tab3_planes[:], list3, "v3_planes")
 
         e2 = [bank("b", u) for u in range(M_TILES)]
 
@@ -255,7 +284,7 @@ def tile_list_bid_pair_board_kernel(
             codes, plane = quantise(round_weight(w3_raw[a], False, vector_quads), "w3_%d" % a)
             for u in range(M_TILES):
                 mx(e2[u], codes[:, cols(u)].bitcast(FP8X4), plane[:, cols(u)],
-                   v_codes[a][:].bitcast(FP8X4), v_planes[4 * a : P, :], start, stop)
+                   v_codes[a][:].bitcast(FP8X4), v_planes[a][:], start, stop)
 
         def table_pass(acc, picked, planes, first_row, b, start, stop):
             codes, plane = h_q[b]
@@ -263,28 +292,26 @@ def tile_list_bid_pair_board_kernel(
                 mx(acc[u], picked[:, cols(u)].bitcast(FP8X4), planes[first_row + 4 * b : P, cols(u)],
                    codes[:].bitcast(FP8X4), plane[:], start, stop)
 
-        h_rows1 = larger_reading(x2_sb1, 1)
-        w3_pass(0, VECTOR_QUADS, True, False)
+        h_rows1 = larger_reading(x1_second, x2_sb1, 1)
+        w3_pass(0, 0, True, False)
         h_grouped1 = interleave_h(h_rows1)
-        table_pass(e2, gather_words(tab2_win[0], list2, "v2_codes0"), v2_planes, 0, 0, False, False)
+        table_pass(e2, gather_words(tab2_win[0], list2, "v2_codes0"), v2_planes, 4, 0, False, False)
         h_q.append(quantise(h_grouped1, "h1"))
-        w3_pass(1, VECTOR_QUADS, False, False)
-        table_pass(e2, gather_words(tab2_win[1], list2, "v2_codes1"), v2_planes, 0, 1, False, False)
+        w3_pass(1, 0, False, False)
+        table_pass(e2, gather_words(tab2_win[1], list2, "v2_codes1"), v2_planes, 4, 1, False, False)
         w3_pass(2, VECTOR_QUADS, False, True)
 
         e3 = [bank("a", u) for u in range(M_TILES)]
         table_pass(e3, gather_words(tab3_win[0], list3, "v3_codes0"), v3_planes, 8, 0, True, False)
-        bounded = []
+        bounded = held([P, M_TILES, S], F32, "x1_sb")
         for u in range(M_TILES):
-            th = held([P, S], F32, "x2_sb0%d" % u)
-            nc.scalar.activation(out=th[:], in_=e2[u][:], func=ACT.Tanh)
-            bounded.append(th)
+            nc.scalar.activation(out=bounded[:, u, :], in_=e2[u][:], func=ACT.Tanh)
         table_pass(e3, gather_words(tab3_win[1], list3, "v3_codes1", pieces=2), v3_planes, 8, 1, False, True)
 
         for u in range(M_TILES):
             larger = held([P, S], F32, "x2_sb1%d" % u)
-            nc.vector.tensor_tensor(out=larger[:], in0=e3[u][:], in1=bounded[u][:], op=ALU.max)
-            score = held([P, S], F32, "score%d" % u)
+            nc.vector.tensor_tensor(out=larger[:], in0=e3[u][:], in1=bounded[:, u, :], op=ALU.max)
+            score = larger
             if u < M_TILES - 1:
                 nc.scalar.activation(out=score[:], in_=larger[:], func=ACT.Copy, scale=gains[:, u : u + 1])
             else:

from contextlib import ExitStack

import concourse.mybir as mybir

K, T, S, H, S2 = 1536, 2048, 512, 1024, 512
FLOPS = 2 * (2 * K * H * S + 2 * H * S2 * S + K * S2 * S)

F32 = mybir.dt.float32
BF16 = mybir.dt.bfloat16
I32 = mybir.dt.int32
U32 = mybir.dt.uint32
U16 = mybir.dt.uint16
U8 = mybir.dt.uint8
FP8X4 = mybir.dt.float8_e4m3fn_x4
FP4X4 = mybir.dt.float4_e2m1fn_x4
ALU = mybir.AluOpType
ACT = mybir.ActivationFunctionType

P = 128
PACK = 4
K_PASS = P * PACK
K_PASSES = K // K_PASS
H_PASSES = H // K_PASS
M_TILES = S2 // P
RAW_BUFS = 8
VECTOR_QUADS = 0


def tile_list_bid_pair_board_kernel(
    tc, tab_words, tab_scales, offs, tab2_words, tab2_scales, offs2, tab3_words, tab3_scales, offs3,
    w1, b1, w2_words, w2_scales, w3, gain, out,
):
    nc = tc.nc
    with ExitStack() as ctx:
        keep = ctx.enter_context(tc.tile_pool(name="keep", bufs=1))
        raw_pool = ctx.enter_context(tc.tile_pool(name="raw", bufs=RAW_BUFS))
        stage = ctx.enter_context(tc.tile_pool(name="stage", bufs=3))
        psum = ctx.enter_context(tc.psum_pool(name="psum", bufs=1))

        def held(shape, dtype, name):
            return keep.tile(shape, dtype, name=name, align_bytes=64)

        def bank(group, index):
            return psum.tile([P, S], F32, name="bank_%s%d" % (group, index))

        def load_list(source, name):
            listed = keep.tile([P, S // 16], U16, name=name)
            nc.sync.dma_start(listed[:], source)
            return listed

        def load_words(words, a, name):
            window = held([P, T], I32, name)
            nc.sync.dma_start(out=window[:], in_=words[a].rearrange("p t i -> p (t i)").bitcast(I32))
            return window

        def load_weight(w, a, b):
            raw = raw_pool.tile([P, PACK, K_PASS], F32, name="raw")
            rows = w[a * K_PASS : (a + 1) * K_PASS, b * K_PASS : (b + 1) * K_PASS]
            nc.sync.dma_start(out=raw[:], in_=rows.rearrange("(p j) c -> p j c", j=PACK))
            return raw

        def zeroed(engine, shape, name):
            planes = held(shape, U8, name)
            engine.memset(planes[:].bitcast(I32), 0)
            return planes

        def load_planes_apart(planes, scales):
            for q in range(4):
                nc.sync.dma_start(
                    out=planes[32 * q : 32 * q + 4, :, :].bitcast(I32),
                    in_=scales[:, 4 * q : 4 * q + 4, :].bitcast(I32).rearrange("a r n -> r a n"),
                )

        def load_planes_packed(planes, scales, first_row):
            rows = 4 * scales.shape[0]
            for q in range(4):
                start = 32 * q + first_row
                nc.gpsimd.dma_start(
                    out=planes[start : start + rows, :].bitcast(I32),
                    in_=scales[:, 4 * q : 4 * q + 4, :].bitcast(I32),
                )

        def gather_words(window, listed, name, pieces=1):
            picked = held([P, S], U32, name)
            step = S // pieces
            for u in range(pieces):
                part = listed[:, u * step // 16 : (u + 1) * step // 16]
                nc.vector.tensor_copy(picked[:, u * step : (u + 1) * step], window[:].bitcast(U32).indirect(part))
            return picked

        def gather_planes(planes, listed, name):
            picked = held([P, S], U8, name)
            nc.vector.tensor_copy(picked[:], planes.indirect(listed[:]))
            return picked

        def round_weight(raw, dealt, vector_quads):
            grouped = stage.tile([P, K_PASS * PACK], BF16, name="grouped", align_bytes=64)
            source = raw[:].rearrange("p j (m t) -> p m j t", t=PACK)
            if dealt:
                target = grouped[:].rearrange("p (t m j) -> p m j t", t=PACK, j=PACK)
            else:
                target = grouped[:].rearrange("p (m t j) -> p m j t", t=PACK, j=PACK)
            cut = P - vector_quads
            nc.scalar.copy(out=target[:, 0:cut], in_=source[:, 0:cut])
            if vector_quads:
                nc.vector.tensor_copy(out=target[:, cut:P], in_=source[:, cut:P])
            return grouped

        def quantise(grouped, name):
            codes = held([P, K_PASS], U32, name + "_codes")
            plane = held([P, K_PASS], U8, name + "_plane")
            nc.vector.quantize_mx(out=codes[:].bitcast(FP8X4), scales=plane[:], in_=grouped[:])
            return codes, plane

        def mx(acc, lhs, lhs_plane, rhs, rhs_plane, start, stop):
            nc.tensor.matmul_mx(
                out=acc[:], lhsT=lhs, lhsT_scale=lhs_plane, rhs=rhs, rhs_scale=rhs_plane, start=start, stop=stop
            )

        def cols(index):
            return slice(index * P, (index + 1) * P)

        tab_planes = zeroed(nc.vector, [P, K_PASSES, T], "tab_planes")
        w2_planes_raw = zeroed(nc.vector, [P, K_PASSES, H], "w2_planes_raw")
        tab2_planes = zeroed(nc.gpsimd, [P, T], "tab2_planes")
        load_planes_packed(tab2_planes, tab2_scales, 4)
        tab3_planes = zeroed(nc.gpsimd, [P, T], "tab3_planes")
        load_planes_packed(tab3_planes, tab3_scales, 8)

        w1_raw = {}
        tab_win = []
        tab_win.append(load_words(tab_words, 0, "tab_win0"))
        list1 = load_list(offs, "list1")
        load_planes_apart(tab_planes, tab_scales)
        w1_raw[0, 0] = load_weight(w1, 0, 0)
        load_planes_apart(w2_planes_raw, w2_scales)
        w2_raw = held([P, K_PASSES, H // 2], I32, "w2_raw")
        nc.sync.dma_start(out=w2_raw[:], in_=w2_words.bitcast(I32).rearrange("a p n -> p a n"))
        tab_win.append(load_words(tab_words, 1, "tab_win1"))
        w1_raw[1, 0] = load_weight(w1, 1, 0)
        tab_win.append(load_words(tab_words, 2, "tab_win2"))
        w1_raw[2, 0] = load_weight(w1, 2, 0)
        bias = keep.tile([P, H_PASSES, PACK], F32, name="bias")
        nc.sync.dma_start(out=bias[:], in_=b1.rearrange("(b p t) -> p b t", p=P, t=PACK))
        w1_raw[0, 1] = load_weight(w1, 0, 1)
        w1_raw[1, 1] = load_weight(w1, 1, 1)
        list2 = load_list(offs2, "list2")
        list3 = load_list(offs3, "list3")
        w1_raw[2, 1] = load_weight(w1, 2, 1)
        gains = keep.tile([P, M_TILES], F32, name="gains")
        with nc.allow_non_contiguous_dma(reason="one gain for each output row"):
            nc.sync.dma_start(out=gains[:], in_=gain.rearrange("(u p) -> p u", p=P))
        w3_raw = [load_weight(w3, 0, 0)]
        tab2_win = [load_words(tab2_words, 0, "tab2_win0")]
        w3_raw.append(load_weight(w3, 1, 0))
        tab2_win.append(load_words(tab2_words, 1, "tab2_win1"))
        w3_raw.append(load_weight(w3, 2, 0))
        tab3_win = [load_words(tab3_words, a, "tab3_win%d" % a) for a in range(H_PASSES)]

        v_codes = []
        v_planes = []
        w1_q = {}

        def x1_pass(x1, a, b):
            codes, plane = w1_q[a, b]
            for t in range(PACK):
                mx(x1[t], codes[:, cols(t)].bitcast(FP8X4), plane[:, cols(t)],
                   v_codes[a][:].bitcast(FP8X4), v_planes[a][:], a == 0, a == K_PASSES - 1)

        def x2_pass(x2, a, b):
            block = a * H_PASSES + b
            for t in range(PACK):
                mx(x2[t], w2_codes[:, t, block * 2 * P : (block + 1) * 2 * P].bitcast(FP4X4), w2_planes[:, t, cols(block)],
                   v_codes[a][:].bitcast(FP8X4), v_planes[a][:], a == 0, a == K_PASSES - 1)

        def x2_pass_by_quarters(x2, a, b):
            block = a * H_PASSES + b
            for q in range(PACK):
                for t in range(PACK):
                    nc.tensor.matmul_mx(
                        out=x2[q][:, cols(t)],
                        lhsT=w2_codes[:, t, block * 2 * P : (block + 1) * 2 * P].bitcast(FP4X4),
                        lhsT_scale=w2_planes[:, t, cols(block)],
                        rhs=v_codes[a][:, cols(q)].bitcast(FP8X4),
                        rhs_scale=v_planes[a][:, cols(q)],
                        start=(a == 0 and t == 0),
                        stop=(a == K_PASSES - 1 and t == PACK - 1),
                    )

        def biased_x1(x1, b):
            x1_sb = held([P, PACK, S], F32, "x1_sb")
            for half in range(2):
                span = slice(half * S // 2, (half + 1) * S // 2)
                for t in range(PACK):
                    nc.scalar.activation(
                        out=x1_sb[:, t, span], in_=x1[t][:, span], func=ACT.Identity, bias=bias[:, b, t : t + 1]
                    )
            return x1_sb

        def larger_interleaved(x2, x1_sb):
            grouped = stage.tile([P, K_PASS * PACK], BF16, name="grouped", align_bytes=64)
            for q in range(PACK):
                nc.vector.tensor_tensor(
                    out=grouped[:, q * K_PASS : (q + 1) * K_PASS].rearrange("p (c i t) -> p c t i", t=PACK, i=4),
                    in0=x2[q][:].rearrange("p (t c i) -> p c t i", t=PACK, i=4),
                    in1=x1_sb[:, :, cols(q)].rearrange("p t (c i) -> p c t i", i=4),
                    op=ALU.max,
                )
            return grouped

        x1_first = [bank("a", t) for t in range(PACK)]
        v_codes.append(gather_words(tab_win[0], list1, "v_codes0"))
        for a in range(K_PASSES):
            v_planes.append(gather_planes(tab_planes[:, a, :], list1, "v_plane%d" % a))
        w1_q[0, 0] = quantise(round_weight(w1_raw[0, 0], True, 0), "w1_00")
        x1_pass(x1_first, 0, 0)
        w2_planes = held([P, PACK, K_PASSES * H // PACK], U8, "w2_planes")
        nc.vector.tensor_copy(
            out=w2_planes[:].rearrange("p t (g i) -> p g t i", i=16),
            in_=w2_planes_raw[:].rearrange("p a (g i t) -> p (a g) t i", t=PACK, i=16),
        )
        w2_codes = held([P, PACK, K_PASSES * H // PACK * 2], U8, "w2_codes")
        nc.vector.tensor_copy(
            out=w2_codes[:].bitcast(U16).rearrange("p t (g i) -> p g t i", i=8),
            in_=w2_raw[:].rearrange("p a n -> p (a n)").bitcast(U16).rearrange("p (g i t) -> p g t i", t=PACK, i=8),
        )
        x2_second = [bank("b", t) for t in range(PACK)]
        x2_pass(x2_second, 0, 1)
        v_codes.append(gather_words(tab_win[1], list1, "v_codes1"))
        x2_pass(x2_second, 1, 1)
        grouped = round_weight(w1_raw[1, 0], True, 0)
        v_codes.append(gather_words(tab_win[2], list1, "v_codes2"))
        x2_pass(x2_second, 2, 1)
        w1_q[1, 0] = quantise(grouped, "w1_10")
        x1_pass(x1_first, 1, 0)

        def empty_x2(x2, b):
            kept = []
            for t in range(PACK):
                x2_sb = held([P, S], F32, "x2_sb%d%d" % (b, t))
                nc.scalar.copy(out=x2_sb[:], in_=x2[t][:])
                kept.append(x2_sb)
            return kept

        def larger_reading(x1, x2_sb, b):
            h_rows = held([P, PACK, S], BF16, "h_rows%d" % b)
            for t in range(PACK):
                nc.vector.scalar_tensor_tensor(
                    out=h_rows[:, t, :], in0=x1[t][:], scalar=bias[:, b, t : t + 1], in1=x2_sb[t][:],
                    op0=ALU.add, op1=ALU.max,
                )
            return h_rows

        def interleave_h(h_rows):
            grouped = stage.tile([P, K_PASS * PACK], BF16, name="grouped", align_bytes=64)
            nc.vector.tensor_copy(
                out=grouped[:].rearrange("p (c i t) -> p c t i", t=PACK, i=4),
                in_=h_rows[:].rearrange("p t (c i) -> p c t i", i=4),
            )
            return grouped

        x2_sb1 = empty_x2(x2_second, 1)
        w1_q[2, 0] = quantise(round_weight(w1_raw[2, 0], True, 2 * VECTOR_QUADS), "w1_20")
        x1_pass(x1_first, 2, 0)
        x2_first = [bank("b", t) for t in range(PACK)]
        for a in range(K_PASSES):
            x2_pass_by_quarters(x2_first, a, 0)
        x1_sb = biased_x1(x1_first, 0)
        x1_second = [bank("a", t) for t in range(PACK)]
        w1_q[0, 1] = quantise(round_weight(w1_raw[0, 1], True, 2 * VECTOR_QUADS), "w1_01")
        x1_pass(x1_second, 0, 1)
        h_grouped0 = larger_interleaved(x2_first, x1_sb)
        w1_q[1, 1] = quantise(round_weight(w1_raw[1, 1], True, VECTOR_QUADS), "w1_11")
        x1_pass(x1_second, 1, 1)
        h_q = [quantise(h_grouped0, "h0")]
        w1_q[2, 1] = quantise(round_weight(w1_raw[2, 1], True, VECTOR_QUADS), "w1_21")
        x1_pass(x1_second, 2, 1)
        v2_planes = gather_planes(tab2_planes[:], list2, "v2_planes")
        v3_planes = gather_planes(tab3_planes[:], list3, "v3_planes")

        e2 = [bank("b", u) for u in range(M_TILES)]

        def w3_pass(a, vector_quads, start, stop):
            codes, plane = quantise(round_weight(w3_raw[a], False, vector_quads), "w3_%d" % a)
            for u in range(M_TILES):
                mx(e2[u], codes[:, cols(u)].bitcast(FP8X4), plane[:, cols(u)],
                   v_codes[a][:].bitcast(FP8X4), v_planes[a][:], start, stop)

        def table_pass(acc, picked, planes, first_row, b, start, stop):
            codes, plane = h_q[b]
            for u in range(M_TILES):
                mx(acc[u], picked[:, cols(u)].bitcast(FP8X4), planes[first_row + 4 * b : P, cols(u)],
                   codes[:].bitcast(FP8X4), plane[:], start, stop)

        h_rows1 = larger_reading(x1_second, x2_sb1, 1)
        w3_pass(0, 0, True, False)
        h_grouped1 = interleave_h(h_rows1)
        table_pass(e2, gather_words(tab2_win[0], list2, "v2_codes0"), v2_planes, 4, 0, False, False)
        h_q.append(quantise(h_grouped1, "h1"))
        w3_pass(1, 0, False, False)
        table_pass(e2, gather_words(tab2_win[1], list2, "v2_codes1"), v2_planes, 4, 1, False, False)
        w3_pass(2, VECTOR_QUADS, False, True)

        e3 = [bank("a", u) for u in range(M_TILES)]
        table_pass(e3, gather_words(tab3_win[0], list3, "v3_codes0"), v3_planes, 8, 0, True, False)
        bounded = held([P, M_TILES, S], F32, "x1_sb")
        for u in range(M_TILES):
            nc.scalar.activation(out=bounded[:, u, :], in_=e2[u][:], func=ACT.Tanh)
        table_pass(e3, gather_words(tab3_win[1], list3, "v3_codes1", pieces=2), v3_planes, 8, 1, False, True)

        for u in range(M_TILES):
            larger = held([P, S], F32, "x2_sb1%d" % u)
            nc.vector.tensor_tensor(out=larger[:], in0=e3[u][:], in1=bounded[:, u, :], op=ALU.max)
            score = larger
            if u < M_TILES - 1:
                nc.scalar.activation(out=score[:], in_=larger[:], func=ACT.Copy, scale=gains[:, u : u + 1])
            else:
                nc.vector.tensor_scalar(out=score[:], in0=larger[:], scalar1=gains[:, u : u + 1], scalar2=None, op0=ALU.mult)
            nc.sync.dma_start(out=out[cols(u), :], in_=score[:])
